import numpy as np
import ml_dtypes


def mxq(x, axis, fmt="e4m3"):
    dtype, down = {"e4m3": (ml_dtypes.float8_e4m3fn, 7), "e5m2": (ml_dtypes.float8_e5m2, 14)}[fmt]
    v = np.moveaxis(np.asarray(x, np.float32).astype(ml_dtypes.bfloat16).astype(np.float64), axis, -1)
    blocks = v.reshape(v.shape[:-1] + (-1, 32))
    amax = np.abs(blocks).max(-1, keepdims=True)
    byte = np.maximum(np.where(amax > 0, np.frexp(amax)[1] - 1 + 127, 0) - down, 1)
    scale = np.exp2(byte - 127.0)
    codes = (blocks / scale).astype(np.float32).astype(dtype).astype(np.float64)
    return np.moveaxis((codes * scale).reshape(v.shape), -1, axis)


WIDE = False


def mx_kscale(k):
    if not WIDE:
        return np.ones(k)
    levels = np.array([10, -10, 5, -5, 0])
    if k % 512:
        return np.exp2(np.random.permutation(np.resize(levels, k // 32))).repeat(32)
    a = np.empty((k // 512, 16))
    for p in range(k // 512):
        a[p, :8] = np.random.permutation(np.resize(levels, 8))
        for g in range(8):
            far = levels[np.abs(levels - a[p, g]) >= 10]
            a[p, g + 8] = far[np.random.randint(len(far))]
    return np.exp2(a.ravel()).repeat(32)


BF16 = ml_dtypes.bfloat16


def bf(x):
    return np.asarray(x, np.float32).astype(BF16)


def f64(x):
    return np.asarray(x).astype(np.float64)

def planes(Y):
    n, m = Y.shape
    b = f64(bf(Y)).reshape(n // 32, 32, m)
    amax = np.abs(b).max(1)
    byte = np.clip(np.where(amax > 0, np.frexp(amax)[1] - 1 + 127 - 7, 1), 1, 254)
    codes = (b * np.exp2(127.0 - byte)[:, None, :]).reshape(n, m).astype(np.float32).astype(ml_dtypes.float8_e4m3fn).view(np.uint8)
    words = codes.reshape(n // 512, 128, 4, m).transpose(0, 1, 3, 2)
    return np.ascontiguousarray(words), np.ascontiguousarray(byte.astype(np.uint8).reshape(n // 512, 16, m))


T, D, R = 512, 2048, 1024


def silu(v):
    return v * (1.0 / (1.0 + np.exp(-v)))


def setup_inputs():
    s, t = mx_kscale(D), mx_kscale(R)
    return {
        "h": bf(np.random.standard_normal((T, D)) * s),
        "rot_in": bf(np.random.standard_normal((R, D)) / np.sqrt(D) / s[None, :]),
        "w": bf(np.random.standard_normal((D, R)) / np.sqrt(D) / s[:, None]),
        "b": bf(0.3 * np.random.standard_normal(R)),
        "g": bf((1.0 + 0.1 * np.random.standard_normal(R)) * t),
        "rot_out": bf(np.random.standard_normal((R, D)) / np.sqrt(R) / t[:, None]),
        "pw": bf(np.random.uniform(0.3, 1.0, T)),
    }


def core(h, rot_in, w, b, g, rot_out, pw):
    hq = mxq(f64(h), 1, "e4m3")
    base = hq @ mxq(f64(rot_in), 1, "e4m3").T
    pre = (hq @ mxq(f64(w), 0, "e4m3")) + f64(b)[None, :]
    src = silu(pre)
    diff = (src - base) * f64(g)[None, :]
    e = mxq(diff, 1, "e4m3") @ mxq(f64(rot_out), 0, "e4m3")
    return f64(pw)[:, None] * e


def reference(h, rot_in, w, b, g, rot_out, pw):
    R_out = core(h, rot_in, w, b, g, rot_out, pw)
    words, scales = planes(R_out)
    return R_out, words, scales

@@ -1,0 +1,383 @@
+from contextlib import ExitStack
+
+import concourse.mybir as mybir
+from concourse.masks import make_identity
+
+T, D, R = 512, 2048, 1024
+
+FLOPS = 2 * T * D * R * 3
+
+F32 = mybir.dt.float32
+BF16 = mybir.dt.bfloat16
+U32 = mybir.dt.uint32
+I32 = mybir.dt.int32
+U8 = mybir.dt.uint8
+FP8X4 = mybir.dt.float8_e4m3fn_x4
+ACT = mybir.ActivationFunctionType
+ALU = mybir.AluOpType
+
+P = 128
+PACK = 4
+K_PASS = P * PACK
+D_PASSES = D // K_PASS
+R_PASSES = R // K_PASS
+N_TILE = 512
+N_CHUNKS = D // N_TILE
+R_TILES = R // P
+
+
+def tile_loreftsubspaceintervention_x1_kernel(tc, h, rot_in, w, b, g, rot_out, pw, out_0, out_1, out_2):
+    nc = tc.nc
+    with ExitStack() as ctx:
+        const = ctx.enter_context(tc.tile_pool(name="const", bufs=1))
+        keep = ctx.enter_context(tc.tile_pool(name="keep", bufs=1))
+        rows = ctx.enter_context(tc.tile_pool(name="rows", bufs=6))
+        wide = ctx.enter_context(tc.tile_pool(name="wide", bufs=4))
+        grouped = ctx.enter_context(tc.tile_pool(name="grouped", bufs=10))
+        rot_pool = ctx.enter_context(tc.tile_pool(name="rot_pool", bufs=4))
+        src_pool = ctx.enter_context(tc.tile_pool(name="src_pool", bufs=4))
+        base_pool = ctx.enter_context(tc.tile_pool(name="base_pool", bufs=8))
+        big = ctx.enter_context(tc.tile_pool(name="big", bufs=4))
+        psum_t = ctx.enter_context(tc.psum_pool(name="psum_t", bufs=2))
+        psum_m = ctx.enter_context(tc.psum_pool(name="psum_m", bufs=6))
+
+        ident = const.tile([P, P], F32, name="ident")
+        make_identity(nc, ident[:])
+
+        h_view = h.rearrange("(m t) k -> t m k", t=PACK)
+        rot_view = rot_in.rearrange("(g m t) k -> g t m k", g=R_PASSES, t=PACK)
+
+        def load_rows(view):
+            row = rows.tile([P, D], BF16, name="row")
+            nc.sync.dma_start(out=row[:], in_=view)
+            return row
+
+        def load_wide(view):
+            raw = wide.tile([P, PACK, 1024], BF16, name="raw")
+            nc.sync.dma_start(out=raw[:], in_=view)
+            return raw
+
+        b_raw = const.tile([P, R_PASSES, PACK], BF16, name="b_raw")
+        g_raw = const.tile([P, R_PASSES, PACK], BF16, name="g_raw")
+        pw_raw = const.tile([P, PACK], BF16, name="pw_raw")
+        nc.scalar.dma_start(out=g_raw[:], in_=g.rearrange("(g m t) -> m g t", g=R_PASSES, t=PACK))
+        nc.scalar.dma_start(out=b_raw[:], in_=b.rearrange("(g m t) -> m g t", g=R_PASSES, t=PACK))
+        nc.scalar.dma_start(out=pw_raw[:], in_=pw.rearrange("(m t) -> m t", t=PACK))
+        b_col = const.tile([P, R_PASSES, PACK], F32, name="b_col")
+        g_col = const.tile([P, R_PASSES, PACK], F32, name="g_col")
+        pw_col = const.tile([P, PACK], F32, name="pw_col")
+        warm = const.tile([P, 1], F32, name="warm")
+        nc.gpsimd.memset(warm[:], 0.0)
+        nc.scalar.activation(out=warm[:], in_=warm[:], func=ACT.Silu)
+        nc.gpsimd.tensor_copy(out=g_col[:], in_=g_raw[:])
+        nc.gpsimd.tensor_copy(out=b_col[:], in_=b_raw[:])
+        nc.gpsimd.tensor_copy(out=pw_col[:], in_=pw_raw[:])
+
+        h_rows = [load_rows(h_view[t]) for t in range(PACK)]
+        rot_rows = {}
+        w_raw = {}
+
+        def load_rot(s):
+            rot_rows[s] = load_rows(rot_view[s // PACK, s % PACK])
+
+        def load_w(c):
+            w_raw[c] = load_wide(w[c * K_PASS : (c + 1) * K_PASS, :].rearrange("(p j) r -> p j r", j=PACK))
+
+        for c in range(D_PASSES):
+            load_rot(2 * c)
+            load_rot(2 * c + 1)
+            load_w(c)
+        ro_raw = {}
+        for half in range(2):
+            for q in range(R_PASSES):
+                ro_raw[q, half] = load_wide(
+                    rot_out[q * K_PASS : (q + 1) * K_PASS, half * 1024 : (half + 1) * 1024].rearrange("(p j) n -> p j n", j=PACK)
+                )
+
+        h_codes = keep.tile([P, D_PASSES, T], U32, name="h_codes", align_bytes=64)
+        h_scales = keep.tile([P, D_PASSES, T], U8, name="h_scales", align_bytes=64)
+        w_codes = keep.tile([P, D_PASSES, R], U32, name="w_codes", align_bytes=64)
+        w_scales = keep.tile([P, D_PASSES, R], U8, name="w_scales", align_bytes=64)
+        ro_codes = keep.tile([P, R_PASSES, D], U32, name="ro_codes", align_bytes=64)
+        ro_scales = keep.tile([P, R_PASSES, D], U8, name="ro_scales", align_bytes=64)
+        d_codes = keep.tile([P, R_PASSES, T], U32, name="d_codes", align_bytes=64)
+        d_scales = keep.tile([P, R_PASSES, T], U8, name="d_scales", align_bytes=64)
+        o_codes = keep.tile([P, D], U32, name="o_codes", align_bytes=64)
+        o_scales = keep.tile([P, D], U8, name="o_scales", align_bytes=64)
+
+        def group_tile():
+            grp = grouped.tile([P, N_TILE, PACK], BF16, name="grp", align_bytes=64)
+            return grp
+
+        def quantize(codes, scales, grp):
+            nc.vector.quantize_mx(out=codes.bitcast(FP8X4), scales=scales, in_=grp[:].rearrange("p w j -> p (w j)"))
+
+        def copy(eng, out, in_):
+            if eng == "S":
+                nc.scalar.copy(out=out, in_=in_)
+            else:
+                nc.vector.tensor_copy(out=out, in_=in_)
+
+        h_grp = {}
+
+        def t_words(bank, slot, row, c):
+            words = row[:].bitcast(F32)
+            for u in range(2):
+                nc.tensor.transpose(bank[:, slot, u, :], words[:, 256 * c + u : 256 * (c + 1) : 2], ident[:])
+
+        def t_bank(kind):
+            if kind == "t":
+                bank = psum_t.tile([P, 2, 2, P], F32, name="bank_t")
+            else:
+                bank = psum_m.tile([P, 2, 2, P], F32, name="bank_m")
+            return bank
+
+        def copy_words(eng, grp, off, bank):
+            dst = grp[:].rearrange("p w j -> p (w j)").bitcast(F32).rearrange("p (s r u) -> p s r u", r=P, u=2)
+            copy(eng, dst[:, off : off + 2], bank[:].rearrange("p s u r -> p s r u"))
+
+        def h_step(tp, c, eng):
+            if tp == 0:
+                h_grp[c] = group_tile()
+            bank = t_bank("m")
+            for i in range(2):
+                t_words(bank, i, h_rows[2 * tp + i], c)
+            copy_words(eng, h_grp[c], 2 * tp, bank)
+
+        def h_quant(c):
+            quantize(h_codes[:, c, :], h_scales[:, c, :], h_grp[c])
+
+        rot_grp = {}
+        rot_codes = {}
+
+        def rot_transpose(s, engs):
+            rot_grp[s] = group_tile()
+            for half in range(2):
+                bank = t_bank("t")
+                for i in range(2):
+                    t_words(bank, i, rot_rows[s], 2 * half + i)
+                copy_words(engs[half], rot_grp[s], 2 * half, bank)
+
+        def rot_quant(s):
+            codes = rot_pool.tile([P, D_PASSES, P], U32, name="r_codes", align_bytes=64)
+            scales = rot_pool.tile([P, D_PASSES, P], U8, name="r_scales", align_bytes=64)
+            quantize(codes[:].rearrange("p c m -> p (c m)"), scales[:].rearrange("p c m -> p (c m)"), rot_grp[s])
+            rot_codes[s] = (codes, scales)
+
+        w_grp = {}
+
+        def w_group(c, gi, s_part):
+            w_grp[c, gi] = group_tile()
+            dst = w_grp[c, gi][:].rearrange("p (t m) j -> p t m j", t=PACK)
+            source = w_raw[c][:, :, gi * 512 : (gi + 1) * 512].rearrange("p j (m t) -> p t m j", t=PACK)
+            cut = P - s_part
+            if cut:
+                nc.vector.tensor_copy(out=dst[:, :, :cut], in_=source[:, :, :cut])
+            if s_part:
+                nc.scalar.copy(out=dst[:, :, cut:], in_=source[:, :, cut:])
+
+        def w_quant(c, gi):
+            cols = slice(gi * 512, (gi + 1) * 512)
+            quantize(w_codes[:, c, cols], w_scales[:, c, cols], w_grp[c, gi])
+
+        ro_grp = {}
+
+        def ro_group(q, n, s_part):
+            ro_grp[q, n] = group_tile()
+            lo = (n % 2) * 512
+            dst = ro_grp[q, n][:].rearrange("p (c i) j -> p c j i", i=4)
+            source = ro_raw[q, n // 2][:, :, lo : lo + 512].rearrange("p j (c i) -> p c j i", i=4)
+            cut = P - s_part
+            if cut:
+                nc.vector.tensor_copy(out=dst[:, :cut], in_=source[:, :cut])
+            if s_part:
+                nc.scalar.copy(out=dst[:, cut:], in_=source[:, cut:])
+
+        def ro_quant(q, n):
+            cols = slice(n * 512, (n + 1) * 512)
+            quantize(ro_codes[:, q, cols], ro_scales[:, q, cols], ro_grp[q, n])
+
+        def mm(acc, lhs, lhs_s, rhs, rhs_s, start, stop):
+            nc.tensor.matmul_mx(
+                out=acc, lhsT=lhs.bitcast(FP8X4), lhsT_scale=lhs_s, rhs=rhs.bitcast(FP8X4), rhs_scale=rhs_s, start=start, stop=stop
+            )
+
+        base = {}
+        src = {}
+        accs = {}
+
+        def mm_bank():
+            acc = psum_m.tile([P, N_TILE], F32, name="bank_m")
+            return acc
+
+        def base_mm(s):
+            acc = mm_bank()
+            codes, scales = rot_codes[s]
+            for c in range(D_PASSES):
+                mm(acc[:], codes[:, c, :], scales[:, c, :], h_codes[:, c, :], h_scales[:, c, :], c == 0, c == D_PASSES - 1)
+            accs["b", s] = acc
+
+        def base_out(s):
+            base[s] = base_pool.tile([P, T], F32, name="base")
+            nc.scalar.activation(out=base[s][:], in_=accs["b", s][:], func=ACT.Copy, scale=g_col[:, s // PACK, s % PACK : s % PACK + 1])
+
+        def pre_mm(s, c):
+            if c == 0:
+                accs["p", s] = mm_bank()
+            cols = slice(s * P, (s + 1) * P)
+            mm(accs["p", s][:], w_codes[:, c, cols], w_scales[:, c, cols], h_codes[:, c, :], h_scales[:, c, :], c == 0, c == D_PASSES - 1)
+
+        def pre_out(s):
+            src[s] = src_pool.tile([P, T], F32, name="src")
+            nc.scalar.activation(out=src[s][:], in_=accs["p", s][:], func=ACT.Silu, bias=b_col[:, s // PACK, s % PACK : s % PACK + 1])
+
+        diff = {}
+
+        def diff_part(s):
+            gi, t = divmod(s, PACK)
+            if t == 0:
+                diff[gi] = big.tile([P, PACK, T], F32, name="big_t")
+            nc.vector.scalar_tensor_tensor(
+                out=diff[gi][:, t, :], in0=src[s][:], scalar=g_col[:, gi, t : t + 1], in1=base[s][:], op0=ALU.mult, op1=ALU.subtract
+            )
+
+        d_grp = {}
+
+        def diff_group(gi):
+            d_grp[gi] = group_tile()
+            nc.vector.tensor_copy(
+                out=d_grp[gi][:].rearrange("p (c i) j -> p c j i", i=4),
+                in_=diff[gi][:].rearrange("p j (c i) -> p c j i", i=4),
+            )
+
+        def diff_quant(gi):
+            quantize(d_codes[:, gi, :], d_scales[:, gi, :], d_grp[gi])
+
+        out_view = out_0.rearrange("(m t) d -> m t d", t=PACK)
+        words_view = out_1[0]
+        res = {}
+
+        def out_mm(n, t, q):
+            if q == 0:
+                if n % 2 == 1 and t >= 2:
+                    acc = psum_t.tile([P, N_TILE], F32, name="bank_t")
+                else:
+                    acc = mm_bank()
+                accs["o", n, t] = acc
+            mm(
+                accs["o", n, t][:],
+                d_codes[:, q, t * P : (t + 1) * P],
+                d_scales[:, q, t * P : (t + 1) * P],
+                ro_codes[:, q, n * 512 : (n + 1) * 512],
+                ro_scales[:, q, n * 512 : (n + 1) * 512],
+                q == 0,
+                q == R_PASSES - 1,
+            )
+
+        def out_copy(n, t, eng):
+            if t == 0:
+                res[n] = big.tile([P, PACK, N_TILE], F32, name="big_t")
+            if eng == "S":
+                nc.scalar.activation(out=res[n][:, t, :], in_=accs["o", n, t][:], func=ACT.Copy, scale=pw_col[:, t : t + 1])
+            else:
+                nc.vector.tensor_scalar(out=res[n][:, t, :], in0=accs["o", n, t][:], scalar1=pw_col[:, t : t + 1], scalar2=None, op0=ALU.mult)
+
+        def out_store(n):
+            nc.sync.dma_start(out=out_view[:, :, n * 512 : (n + 1) * 512], in_=res[n][:])
+
+        o_grp = {}
+
+        def out_group(n):
+            o_grp[n] = group_tile()
+            nc.vector.tensor_copy(
+                out=o_grp[n][:].rearrange("p (c i) j -> p c j i", i=4),
+                in_=res[n][:].rearrange("p j (c i) -> p c j i", i=4),
+            )
+
+        def out_quant(n):
+            cols = slice(n * 512, (n + 1) * 512)
+            quantize(o_codes[:, cols], o_scales[:, cols], o_grp[n])
+
+        def words_store(n):
+            cols = slice(n * 512, (n + 1) * 512)
+            nc.sync.dma_start(out=words_view[:, cols, :].rearrange("p m t -> p (m t)").bitcast(I32), in_=o_codes[:, cols].bitcast(I32))
+
+        def scales_store(lo, hi):
+            for q in range(4):
+                nc.sync.dma_start(
+                    out=out_2[0][4 * q : 4 * q + 4, lo:hi].bitcast(I32), in_=o_scales[32 * q : 32 * q + 4, lo:hi].bitcast(I32)
+                )
+
+        with tc.manual_schedule():
+            for tp in range(2):
+                for c in range(D_PASSES):
+                    h_step(tp, c, "S" if c % 2 == 0 else "V")
+                    if tp == 1 and c >= 1:
+                        h_quant(c - 1)
+            rot_transpose(0, "SS")
+            h_quant(D_PASSES - 1)
+            rot_transpose(1, "SV")
+            rot_quant(0)
+            for s in range(2, R_TILES + 2):
+                c, gi = divmod(s - 2, 2)
+                if s < R_TILES:
+                    rot_transpose(s, "SS")
+                w_group(c, gi, 32)
+                rot_quant(s - 1) if s <= R_TILES else None
+                base_mm(s - 2)
+                base_out(s - 2)
+                w_quant(c, gi)
+                if gi == 1:
+                    for i in range(PACK):
+                        pre_mm(i, c)
+            ro_group(0, 0, 32)
+            for s in range(PACK):
+                pre_out(s)
+                for c in range(D_PASSES):
+                    pre_mm(s + PACK, c)
+            ro_quant(0, 0)
+            for s in range(PACK):
+                diff_part(s)
+            ro_group(1, 0, 32)
+            diff_group(0)
+            ro_quant(1, 0)
+            diff_quant(0)
+            ro_group(0, 1, 32)
+            for s in range(PACK, 2 * PACK):
+                pre_out(s)
+                diff_part(s)
+            ro_quant(0, 1)
+            ro_group(1, 1, 48)
+            diff_group(1)
+            for n in range(2):
+                for t in range(PACK):
+                    out_mm(n, t, 0)
+            ro_quant(1, 1)
+            diff_quant(1)
+            ro_group(0, 2, 32)
+            ro_group(1, 2, 32)
+            ro_quant(0, 2)
+            ro_quant(1, 2)
+            for n in range(N_CHUNKS):
+                for t in range(PACK):
+                    if n >= 2:
+                        out_mm(n, t, 0)
+                    out_mm(n, t, 1)
+                    out_copy(n, t, "V" if (t == 3 and n % 2 == 1) else "S")
+                out_store(n)
+                if n == 0:
+                    ro_group(0, 3, 32)
+                    ro_group(1, 3, 32)
+                    ro_quant(0, 3)
+                    ro_quant(1, 3)
+                if n >= 1:
+                    out_group(n - 1)
+                if n >= 2:
+                    out_quant(n - 2)
+                    words_store(n - 2)
+            out_group(N_CHUNKS - 1)
+            out_quant(N_CHUNKS - 2)
+            words_store(N_CHUNKS - 2)
+            out_quant(N_CHUNKS - 1)
+            words_store(N_CHUNKS - 1)
+            scales_store(0, D)

@@ -24,6 +24,7 @@ R_PASSES = R // K_PASS
 N_TILE = 512
 N_CHUNKS = D // N_TILE
 R_TILES = R // P
+CHUNKS = ((0,512),(512,1024),(1024,1536),(1536,1792),(1792,2048))
 
 
 def tile_loreftsubspaceintervention_x1_kernel(tc, h, rot_in, w, b, g, rot_out, pw, out_0, out_1, out_2):
@@ -31,8 +32,8 @@ def tile_loreftsubspaceintervention_x1_kernel(tc, h, rot_in, w, b, g, rot_out, p
     with ExitStack() as ctx:
         const = ctx.enter_context(tc.tile_pool(name="const", bufs=1))
         keep = ctx.enter_context(tc.tile_pool(name="keep", bufs=1))
-        rows = ctx.enter_context(tc.tile_pool(name="rows", bufs=6))
-        wide = ctx.enter_context(tc.tile_pool(name="wide", bufs=4))
+        rows = ctx.enter_context(tc.tile_pool(name="rows", bufs=8))
+        wide = ctx.enter_context(tc.tile_pool(name="wide", bufs=3))
         grouped = ctx.enter_context(tc.tile_pool(name="grouped", bufs=10))
         rot_pool = ctx.enter_context(tc.tile_pool(name="rot_pool", bufs=4))
         src_pool = ctx.enter_context(tc.tile_pool(name="src_pool", bufs=4))
@@ -52,11 +53,6 @@ def tile_loreftsubspaceintervention_x1_kernel(tc, h, rot_in, w, b, g, rot_out, p
             nc.sync.dma_start(out=row[:], in_=view)
             return row
 
-        def load_wide(view):
-            raw = wide.tile([P, PACK, 1024], BF16, name="raw")
-            nc.sync.dma_start(out=raw[:], in_=view)
-            return raw
-
         b_raw = const.tile([P, R_PASSES, PACK], BF16, name="b_raw")
         g_raw = const.tile([P, R_PASSES, PACK], BF16, name="g_raw")
         pw_raw = const.tile([P, PACK], BF16, name="pw_raw")
@@ -73,26 +69,55 @@ def tile_loreftsubspaceintervention_x1_kernel(tc, h, rot_in, w, b, g, rot_out, p
         nc.gpsimd.tensor_copy(out=b_col[:], in_=b_raw[:])
         nc.gpsimd.tensor_copy(out=pw_col[:], in_=pw_raw[:])
 
-        h_rows = [load_rows(h_view[t]) for t in range(PACK)]
+        h_rows = {}
         rot_rows = {}
         w_raw = {}
+        ro_raw = {}
+
+        def load_h(t):
+            h_rows[t] = load_rows(h_view[t])
 
         def load_rot(s):
             rot_rows[s] = load_rows(rot_view[s // PACK, s % PACK])
 
         def load_w(c):
-            w_raw[c] = load_wide(w[c * K_PASS : (c + 1) * K_PASS, :].rearrange("(p j) r -> p j r", j=PACK))
+            raw = wide.tile([P, PACK, R], BF16, name="raw")
+            nc.sync.dma_start(out=raw[:], in_=w[c * K_PASS : (c + 1) * K_PASS, :].rearrange("(p j) r -> p j r", j=PACK))
+            for gi in range(R_PASSES):
+                w_raw[c, gi] = raw[:, :, gi * K_PASS : (gi + 1) * K_PASS]
 
-        for c in range(D_PASSES):
-            load_rot(2 * c)
-            load_rot(2 * c + 1)
-            load_w(c)
-        ro_raw = {}
+        def load_w_half(c, gi):
+            row = rows.tile([P, PACK, K_PASS], BF16, name="row")
+            nc.sync.dma_start(
+                out=row[:], in_=w[c * K_PASS : (c + 1) * K_PASS, gi * K_PASS : (gi + 1) * K_PASS].rearrange("(p j) r -> p j r", j=PACK)
+            )
+            w_raw[c, gi] = row[:]
+
+        def load_ro(q, half):
+            ro_raw[q, half] = wide.tile([P, PACK, 1024], BF16, name="raw")
+            nc.sync.dma_start(
+                out=ro_raw[q, half][:],
+                in_=rot_out[q * K_PASS : (q + 1) * K_PASS, half * 1024 : (half + 1) * 1024].rearrange("(p j) n -> p j n", j=PACK),
+            )
+
+        for t in range(PACK):
+            load_h(t)
+        load_rot(0)
+        load_w_half(0, 0)
+        load_rot(1)
+        load_w_half(0, 1)
+        load_rot(2)
+        load_w(1)
+        load_rot(3)
+        load_w(2)
+        load_rot(4)
+        load_rot(5)
+        load_w(3)
+        load_rot(6)
+        load_rot(7)
         for half in range(2):
             for q in range(R_PASSES):
-                ro_raw[q, half] = load_wide(
-                    rot_out[q * K_PASS : (q + 1) * K_PASS, half * 1024 : (half + 1) * 1024].rearrange("(p j) n -> p j n", j=PACK)
-                )
+                load_ro(q, half)
 
         h_codes = keep.tile([P, D_PASSES, T], U32, name="h_codes", align_bytes=64)
         h_scales = keep.tile([P, D_PASSES, T], U8, name="h_scales", align_bytes=64)
@@ -136,13 +161,22 @@ def tile_loreftsubspaceintervention_x1_kernel(tc, h, rot_in, w, b, g, rot_out, p
             dst = grp[:].rearrange("p w j -> p (w j)").bitcast(F32).rearrange("p (s r u) -> p s r u", r=P, u=2)
             copy(eng, dst[:, off : off + 2], bank[:].rearrange("p s u r -> p s r u"))
 
-        def h_step(tp, c, eng):
-            if tp == 0:
-                h_grp[c] = group_tile()
+        banks = {}
+
+        def h_transpose(t, cp):
             bank = t_bank("m")
             for i in range(2):
-                t_words(bank, i, h_rows[2 * tp + i], c)
-            copy_words(eng, h_grp[c], 2 * tp, bank)
+                c = 2 * cp + i
+                if c not in h_grp:
+                    h_grp[c] = group_tile()
+                t_words(bank, i, h_rows[t], c)
+            banks["h", t, cp] = bank
+
+        def h_copy(t, cp, eng):
+            bank = banks["h", t, cp]
+            for i in range(2):
+                dst = h_grp[2 * cp + i][:].rearrange("p w j -> p (w j)").bitcast(F32).rearrange("p (s r u) -> p s r u", r=P, u=2)
+                copy(eng, dst[:, t], bank[:, i].rearrange("p u r -> p r u"))
 
         def h_quant(c):
             quantize(h_codes[:, c, :], h_scales[:, c, :], h_grp[c])
@@ -150,13 +184,16 @@ def tile_loreftsubspaceintervention_x1_kernel(tc, h, rot_in, w, b, g, rot_out, p
         rot_grp = {}
         rot_codes = {}
 
-        def rot_transpose(s, engs):
-            rot_grp[s] = group_tile()
-            for half in range(2):
-                bank = t_bank("t")
-                for i in range(2):
-                    t_words(bank, i, rot_rows[s], 2 * half + i)
-                copy_words(engs[half], rot_grp[s], 2 * half, bank)
+        def rot_transpose(s, half):
+            if half == 0:
+                rot_grp[s] = group_tile()
+            bank = t_bank("t")
+            for i in range(2):
+                t_words(bank, i, rot_rows[s], 2 * half + i)
+            banks["r", s, half] = bank
+
+        def rot_copy(s, half, eng):
+            copy_words(eng, rot_grp[s], 2 * half, banks["r", s, half])
 
         def rot_quant(s):
             codes = rot_pool.tile([P, D_PASSES, P], U32, name="r_codes", align_bytes=64)
@@ -166,15 +203,14 @@ def tile_loreftsubspaceintervention_x1_kernel(tc, h, rot_in, w, b, g, rot_out, p
 
         w_grp = {}
 
-        def w_group(c, gi, s_part):
-            w_grp[c, gi] = group_tile()
+        def w_group(c, gi, eng, s_part):
+            if (c, gi) not in w_grp:
+                w_grp[c, gi] = group_tile()
             dst = w_grp[c, gi][:].rearrange("p (t m) j -> p t m j", t=PACK)
-            source = w_raw[c][:, :, gi * 512 : (gi + 1) * 512].rearrange("p j (m t) -> p t m j", t=PACK)
-            cut = P - s_part
-            if cut:
-                nc.vector.tensor_copy(out=dst[:, :, :cut], in_=source[:, :, :cut])
-            if s_part:
-                nc.scalar.copy(out=dst[:, :, cut:], in_=source[:, :, cut:])
+            source = w_raw[c, gi].rearrange("p j (m t) -> p t m j", t=PACK)
+            cols = slice(0, P - s_part) if eng == "V" else slice(P - s_part, P)
+            if cols.start < cols.stop:
+                copy(eng, dst[:, :, cols], source[:, :, cols])
 
         def w_quant(c, gi):
             cols = slice(gi * 512, (gi + 1) * 512)
@@ -182,16 +218,15 @@ def tile_loreftsubspaceintervention_x1_kernel(tc, h, rot_in, w, b, g, rot_out, p
 
         ro_grp = {}
 
-        def ro_group(q, n, s_part):
-            ro_grp[q, n] = group_tile()
+        def ro_group(q, n, eng, s_part):
+            if (q, n) not in ro_grp:
+                ro_grp[q, n] = group_tile()
             lo = (n % 2) * 512
             dst = ro_grp[q, n][:].rearrange("p (c i) j -> p c j i", i=4)
             source = ro_raw[q, n // 2][:, :, lo : lo + 512].rearrange("p j (c i) -> p c j i", i=4)
-            cut = P - s_part
-            if cut:
-                nc.vector.tensor_copy(out=dst[:, :cut], in_=source[:, :cut])
-            if s_part:
-                nc.scalar.copy(out=dst[:, cut:], in_=source[:, cut:])
+            cols = slice(0, P - s_part) if eng == "V" else slice(P - s_part, P)
+            if cols.start < cols.stop:
+                copy(eng, dst[:, cols], source[:, cols])
 
         def ro_quant(q, n):
             cols = slice(n * 512, (n + 1) * 512)
@@ -256,51 +291,63 @@ def tile_loreftsubspaceintervention_x1_kernel(tc, h, rot_in, w, b, g, rot_out, p
         out_view = out_0.rearrange("(m t) d -> m t d", t=PACK)
         words_view = out_1[0]
         res = {}
+        n_alloc = [0]
 
         def out_mm(n, t, q):
+            lo, hi = CHUNKS[n]
             if q == 0:
-                if n % 2 == 1 and t >= 2:
+                use_t = n_alloc[0] % 8 >= 6
+                n_alloc[0] += 1
+                if use_t:
                     acc = psum_t.tile([P, N_TILE], F32, name="bank_t")
                 else:
                     acc = mm_bank()
                 accs["o", n, t] = acc
             mm(
-                accs["o", n, t][:],
+                accs["o", n, t][:, : hi - lo],
                 d_codes[:, q, t * P : (t + 1) * P],
                 d_scales[:, q, t * P : (t + 1) * P],
-                ro_codes[:, q, n * 512 : (n + 1) * 512],
-                ro_scales[:, q, n * 512 : (n + 1) * 512],
+                ro_codes[:, q, lo:hi],
+                ro_scales[:, q, lo:hi],
                 q == 0,
                 q == R_PASSES - 1,
             )
 
         def out_copy(n, t, eng):
-            if t == 0:
+            lo, hi = CHUNKS[n]
+            if n not in res:
                 res[n] = big.tile([P, PACK, N_TILE], F32, name="big_t")
+            dst = res[n][:, t, : hi - lo]
+            acc = accs["o", n, t][:, : hi - lo]
             if eng == "S":
-                nc.scalar.activation(out=res[n][:, t, :], in_=accs["o", n, t][:], func=ACT.Copy, scale=pw_col[:, t : t + 1])
+                nc.scalar.activation(out=dst, in_=acc, func=ACT.Copy, scale=pw_col[:, t : t + 1])
             else:
-                nc.vector.tensor_scalar(out=res[n][:, t, :], in0=accs["o", n, t][:], scalar1=pw_col[:, t : t + 1], scalar2=None, op0=ALU.mult)
+                nc.vector.tensor_scalar(out=dst, in0=acc, scalar1=pw_col[:, t : t + 1], scalar2=None, op0=ALU.mult)
+            done = out_done.setdefault(n, [])
+            done.append(t)
+            if len(done) in (2, 4) and sorted(done[-2:]) in ([0, 1], [2, 3]):
+                t0 = min(done[-2:])
+                nc.sync.dma_start(out=out_view[:, t0 : t0 + 2, lo:hi], in_=res[n][:, t0 : t0 + 2, : hi - lo])
+            elif len(done) == 4:
+                nc.sync.dma_start(out=out_view[:, :, lo:hi], in_=res[n][:, :, : hi - lo])
 
-        def out_store(n):
-            nc.sync.dma_start(out=out_view[:, :, n * 512 : (n + 1) * 512], in_=res[n][:])
-
+        out_done = {}
         o_grp = {}
 
         def out_group(n):
+            lo, hi = CHUNKS[n]
             o_grp[n] = group_tile()
             nc.vector.tensor_copy(
-                out=o_grp[n][:].rearrange("p (c i) j -> p c j i", i=4),
-                in_=res[n][:].rearrange("p j (c i) -> p c j i", i=4),
+                out=o_grp[n][:, : hi - lo].rearrange("p (c i) j -> p c j i", i=4),
+                in_=res[n][:, :, : hi - lo].rearrange("p j (c i) -> p c j i", i=4),
             )
 
         def out_quant(n):
-            cols = slice(n * 512, (n + 1) * 512)
-            quantize(o_codes[:, cols], o_scales[:, cols], o_grp[n])
-
-        def words_store(n):
-            cols = slice(n * 512, (n + 1) * 512)
-            nc.sync.dma_start(out=words_view[:, cols, :].rearrange("p m t -> p (m t)").bitcast(I32), in_=o_codes[:, cols].bitcast(I32))
+            lo, hi = CHUNKS[n]
+            nc.vector.quantize_mx(
+                out=o_codes[:, lo:hi].bitcast(FP8X4), scales=o_scales[:, lo:hi], in_=o_grp[n][:, : hi - lo].rearrange("p w j -> p (w j)")
+            )
+            nc.sync.dma_start(out=words_view[:, lo:hi, :].rearrange("p m t -> p (m t)").bitcast(I32), in_=o_codes[:, lo:hi].bitcast(I32))
 
         def scales_store(lo, hi):
             for q in range(4):
@@ -309,75 +356,247 @@ def tile_loreftsubspaceintervention_x1_kernel(tc, h, rot_in, w, b, g, rot_out, p
                 )
 
         with tc.manual_schedule():
-            for tp in range(2):
-                for c in range(D_PASSES):
-                    h_step(tp, c, "S" if c % 2 == 0 else "V")
-                    if tp == 1 and c >= 1:
-                        h_quant(c - 1)
-            rot_transpose(0, "SS")
-            h_quant(D_PASSES - 1)
-            rot_transpose(1, "SV")
+            h_transpose(0, 0)
+            h_transpose(0, 1)
+            h_copy(0, 0, "V")
+            h_transpose(1, 0)
+            h_copy(0, 1, "S")
+            h_transpose(1, 1)
+            h_copy(1, 0, "V")
+            h_transpose(2, 0)
+            h_copy(1, 1, "S")
+            h_transpose(2, 1)
+            h_copy(2, 0, "V")
+            h_transpose(3, 0)
+            h_copy(2, 1, "S")
+            h_transpose(3, 1)
+            h_copy(3, 0, "V")
+            rot_transpose(0, 0)
+            h_copy(3, 1, "S")
+            h_quant(0)
+            rot_transpose(0, 1)
+            rot_copy(0, 0, "S")
+            w_group(0, 0, "V", 16)
+            rot_copy(0, 1, "S")
+            w_group(0, 0, "S", 16)
+            rot_transpose(1, 0)
+            w_quant(0, 0)
+            rot_transpose(1, 1)
+            h_quant(1)
+            rot_copy(1, 0, "S")
+            pre_mm(0, 0)
+            rot_copy(1, 1, "S")
+            h_quant(2)
+            pre_mm(1, 0)
+            pre_mm(2, 0)
+            w_group(0, 1, "S", 80)
             rot_quant(0)
-            for s in range(2, R_TILES + 2):
-                c, gi = divmod(s - 2, 2)
-                if s < R_TILES:
-                    rot_transpose(s, "SS")
-                w_group(c, gi, 32)
-                rot_quant(s - 1) if s <= R_TILES else None
-                base_mm(s - 2)
-                base_out(s - 2)
-                w_quant(c, gi)
-                if gi == 1:
-                    for i in range(PACK):
-                        pre_mm(i, c)
-            ro_group(0, 0, 32)
-            for s in range(PACK):
-                pre_out(s)
-                for c in range(D_PASSES):
-                    pre_mm(s + PACK, c)
-            ro_quant(0, 0)
-            for s in range(PACK):
-                diff_part(s)
-            ro_group(1, 0, 32)
+            pre_mm(3, 0)
+            rot_transpose(2, 0)
+            h_quant(3)
+            rot_transpose(2, 1)
+            w_group(0, 1, "V", 80)
+            rot_copy(2, 0, "S")
+            base_mm(0)
+            rot_quant(1)
+            rot_copy(2, 1, "S")
+            w_quant(0, 1)
+            w_group(1, 0, "S", 48)
+            base_mm(1)
+            w_group(1, 0, "V", 48)
+            base_out(0)
+            w_quant(1, 0)
+            rot_transpose(3, 0)
+            w_group(1, 1, "S", 48)
+            w_group(1, 1, "V", 48)
+            rot_transpose(3, 1)
+            base_out(1)
+            pre_mm(0, 1)
+            rot_quant(2)
+            pre_mm(1, 1)
+            rot_copy(3, 0, "S")
+            pre_mm(2, 1)
+            w_quant(1, 1)
+            base_mm(2)
+            rot_copy(3, 1, "S")
+            w_group(2, 0, "V", 48)
+            w_group(2, 0, "S", 48)
+            pre_mm(3, 1)
+            rot_quant(3)
+            rot_transpose(4, 0)
+            w_group(2, 1, "S", 32)
+            w_group(2, 1, "V", 32)
+            rot_transpose(4, 1)
+            base_out(2)
+            base_mm(3)
+            rot_copy(4, 0, "S")
+            w_quant(2, 0)
+            rot_copy(4, 1, "S")
+            w_quant(2, 1)
+            rot_transpose(5, 0)
+            base_out(3)
+            rot_quant(4)
+            rot_transpose(5, 1)
+            w_group(3, 0, "S", 32)
+            w_group(3, 0, "V", 32)
+            pre_mm(0, 2)
+            rot_copy(5, 0, "S")
+            pre_mm(1, 2)
+            pre_mm(2, 2)
+            w_group(3, 1, "V", 32)
+            rot_copy(5, 1, "S")
+            rot_transpose(6, 0)
+            w_group(3, 1, "S", 32)
+            rot_transpose(6, 1)
+            w_quant(3, 0)
+            rot_copy(6, 0, "S")
+            pre_mm(3, 2)
+            rot_quant(5)
+            pre_mm(0, 3)
+            rot_copy(6, 1, "S")
+            pre_mm(1, 3)
+            w_quant(3, 1)
+            pre_mm(2, 3)
+            pre_out(0)
+            rot_quant(6)
+            rot_transpose(7, 0)
+            pre_out(1)
+            rot_transpose(7, 1)
+            diff_part(0)
+            rot_copy(7, 0, "S")
+            ro_group(0, 0, "V", 0)
+            pre_mm(3, 3)
+            rot_copy(7, 1, "S")
+            pre_mm(4, 0)
+            pre_mm(4, 1)
+            pre_mm(4, 2)
+            pre_mm(4, 3)
+            pre_out(2)
+            diff_part(1)
+            pre_out(3)
+            base_mm(4)
+            diff_part(2)
+            ro_group(1, 0, "S", 128)
+            ro_group(0, 1, "V", 32)
+            base_mm(5)
+            diff_part(3)
+            pre_mm(5, 0)
+            pre_mm(5, 1)
+            pre_mm(5, 2)
+            pre_mm(5, 3)
+            ro_group(1, 1, "V", 48)
+            base_out(4)
+            rot_quant(7)
+            ro_group(0, 1, "S", 32)
+            pre_mm(6, 0)
+            pre_mm(6, 1)
+            pre_mm(6, 2)
+            pre_mm(6, 3)
             diff_group(0)
+            pre_out(4)
+            ro_group(1, 1, "S", 48)
+            base_mm(6)
+            ro_quant(0, 0)
+            base_out(5)
+            diff_part(4)
+            base_mm(7)
             ro_quant(1, 0)
+            pre_out(5)
+            pre_out(6)
             diff_quant(0)
-            ro_group(0, 1, 32)
-            for s in range(PACK, 2 * PACK):
-                pre_out(s)
-                diff_part(s)
+            pre_mm(7, 0)
+            pre_mm(7, 1)
+            pre_mm(7, 2)
+            pre_mm(7, 3)
+            base_out(6)
+            diff_part(5)
+            base_out(7)
             ro_quant(0, 1)
-            ro_group(1, 1, 48)
+            out_mm(0, 0, 0)
+            out_mm(0, 1, 0)
+            pre_out(7)
+            diff_part(6)
+            out_mm(0, 2, 0)
+            out_mm(0, 3, 0)
+            ro_group(0, 2, "S", 128)
+            diff_part(7)
+            out_mm(1, 0, 0)
+            out_mm(1, 1, 0)
             diff_group(1)
-            for n in range(2):
-                for t in range(PACK):
-                    out_mm(n, t, 0)
-            ro_quant(1, 1)
+            out_mm(1, 2, 0)
+            out_mm(1, 3, 0)
             diff_quant(1)
-            ro_group(0, 2, 32)
-            ro_group(1, 2, 32)
+            ro_group(1, 2, "S", 64)
+            ro_group(1, 2, "V", 64)
+            out_mm(0, 0, 1)
+            out_mm(0, 1, 1)
+            ro_group(0, 3, "V", 16)
+            out_mm(0, 2, 1)
+            out_copy(0, 0, "S")
+            out_mm(0, 3, 1)
+            out_copy(0, 1, "S")
+            ro_quant(1, 1)
+            out_copy(0, 2, "S")
             ro_quant(0, 2)
+            out_mm(1, 0, 1)
+            out_copy(0, 3, "S")
+            out_mm(1, 1, 1)
             ro_quant(1, 2)
-            for n in range(N_CHUNKS):
-                for t in range(PACK):
-                    if n >= 2:
-                        out_mm(n, t, 0)
-                    out_mm(n, t, 1)
-                    out_copy(n, t, "V" if (t == 3 and n % 2 == 1) else "S")
-                out_store(n)
-                if n == 0:
-                    ro_group(0, 3, 32)
-                    ro_group(1, 3, 32)
-                    ro_quant(0, 3)
-                    ro_quant(1, 3)
-                if n >= 1:
-                    out_group(n - 1)
-                if n >= 2:
-                    out_quant(n - 2)
-                    words_store(n - 2)
-            out_group(N_CHUNKS - 1)
-            out_quant(N_CHUNKS - 2)
-            words_store(N_CHUNKS - 2)
-            out_quant(N_CHUNKS - 1)
-            words_store(N_CHUNKS - 1)
+            out_mm(1, 2, 1)
+            out_copy(1, 0, "S")
+            out_mm(1, 3, 1)
+            out_group(0)
+            out_mm(2, 0, 0)
+            out_copy(1, 1, "S")
+            out_mm(2, 0, 1)
+            out_mm(2, 1, 0)
+            out_copy(1, 2, "S")
+            out_mm(2, 1, 1)
+            out_mm(2, 2, 0)
+            ro_group(1, 3, "V", 24)
+            out_copy(1, 3, "S")
+            out_mm(2, 2, 1)
+            out_mm(2, 3, 0)
+            out_copy(2, 0, "S")
+            out_mm(2, 3, 1)
+            out_quant(0)
+            ro_group(0, 3, "S", 16)
+            ro_group(1, 3, "S", 24)
+            ro_quant(0, 3)
+            out_copy(2, 1, "S")
+            ro_quant(1, 3)
+            out_mm(3, 0, 0)
+            out_copy(2, 2, "S")
+            out_group(1)
+            out_mm(3, 0, 1)
+            out_mm(3, 1, 0)
+            out_copy(2, 3, "S")
+            out_mm(3, 1, 1)
+            out_mm(3, 2, 0)
+            out_mm(3, 2, 1)
+            out_mm(3, 3, 0)
+            out_copy(3, 0, "S")
+            out_mm(3, 3, 1)
+            out_mm(4, 0, 0)
+            out_group(2)
+            out_copy(3, 1, "S")
+            out_mm(4, 0, 1)
+            out_mm(4, 1, 0)
+            out_copy(3, 2, "S")
+            out_mm(4, 1, 1)
+            out_mm(4, 2, 0)
+            out_copy(3, 3, "S")
+            out_mm(4, 2, 1)
+            out_mm(4, 3, 0)
+            out_copy(4, 0, "S")
+            out_mm(4, 3, 1)
+            out_quant(1)
+            out_copy(4, 1, "S")
+            out_copy(4, 2, "S")
+            out_group(3)
+            out_copy(4, 3, "S")
+            out_quant(2)
+            out_group(4)
+            out_quant(3)
+            out_quant(4)
             scales_store(0, D)

@@ -24,7 +24,7 @@ R_PASSES = R // K_PASS
 N_TILE = 512
 N_CHUNKS = D // N_TILE
 R_TILES = R // P
-CHUNKS = ((0,512),(512,1024),(1024,1536),(1536,1792),(1792,2048))
+CHUNKS = ((0,512),(512,1024),(1024,1536),(1536,2048))
 
 
 def tile_loreftsubspaceintervention_x1_kernel(tc, h, rot_in, w, b, g, rot_out, pw, out_0, out_1, out_2):
@@ -32,8 +32,8 @@ def tile_loreftsubspaceintervention_x1_kernel(tc, h, rot_in, w, b, g, rot_out, p
     with ExitStack() as ctx:
         const = ctx.enter_context(tc.tile_pool(name="const", bufs=1))
         keep = ctx.enter_context(tc.tile_pool(name="keep", bufs=1))
-        rows = ctx.enter_context(tc.tile_pool(name="rows", bufs=8))
-        wide = ctx.enter_context(tc.tile_pool(name="wide", bufs=3))
+        rows = ctx.enter_context(tc.tile_pool(name="rows", bufs=6))
+        wide = ctx.enter_context(tc.tile_pool(name="wide", bufs=4))
         grouped = ctx.enter_context(tc.tile_pool(name="grouped", bufs=10))
         rot_pool = ctx.enter_context(tc.tile_pool(name="rot_pool", bufs=4))
         src_pool = ctx.enter_context(tc.tile_pool(name="src_pool", bufs=4))
@@ -103,16 +103,10 @@ def tile_loreftsubspaceintervention_x1_kernel(tc, h, rot_in, w, b, g, rot_out, p
         for t in range(PACK):
             load_h(t)
         load_rot(0)
-        load_w_half(0, 0)
         load_rot(1)
-        load_w_half(0, 1)
-        load_rot(2)
-        load_w(1)
-        load_rot(3)
-        load_w(2)
-        load_rot(4)
-        load_rot(5)
-        load_w(3)
+        for c in range(D_PASSES):
+            load_rot(c + 2)
+            load_w(c)
         load_rot(6)
         load_rot(7)
         for half in range(2):
@@ -334,13 +328,15 @@ def tile_loreftsubspaceintervention_x1_kernel(tc, h, rot_in, w, b, g, rot_out, p
         out_done = {}
         o_grp = {}
 
-        def out_group(n):
+        def out_group(n, eng, s_part):
             lo, hi = CHUNKS[n]
-            o_grp[n] = group_tile()
-            nc.vector.tensor_copy(
-                out=o_grp[n][:, : hi - lo].rearrange("p (c i) j -> p c j i", i=4),
-                in_=res[n][:, :, : hi - lo].rearrange("p j (c i) -> p c j i", i=4),
-            )
+            if n not in o_grp:
+                o_grp[n] = group_tile()
+            dst = o_grp[n][:, : hi - lo].rearrange("p (c i) j -> p c j i", i=4)
+            source = res[n][:, :, : hi - lo].rearrange("p j (c i) -> p c j i", i=4)
+            cols = slice(0, P - s_part) if eng == "V" else slice(P - s_part, P)
+            if cols.start < cols.stop:
+                copy(eng, dst[:, cols], source[:, cols])
 
         def out_quant(n):
             lo, hi = CHUNKS[n]
@@ -355,248 +351,120 @@ def tile_loreftsubspaceintervention_x1_kernel(tc, h, rot_in, w, b, g, rot_out, p
                     out=out_2[0][4 * q : 4 * q + 4, lo:hi].bitcast(I32), in_=o_scales[32 * q : 32 * q + 4, lo:hi].bitcast(I32)
                 )
 
+        WS = [[0, 24], [40, 40], [40, 40], [40, 32]]
+        OS = [0,0,0,48]
         with tc.manual_schedule():
-            h_transpose(0, 0)
-            h_transpose(0, 1)
-            h_copy(0, 0, "V")
-            h_transpose(1, 0)
-            h_copy(0, 1, "S")
-            h_transpose(1, 1)
-            h_copy(1, 0, "V")
-            h_transpose(2, 0)
-            h_copy(1, 1, "S")
-            h_transpose(2, 1)
-            h_copy(2, 0, "V")
-            h_transpose(3, 0)
-            h_copy(2, 1, "S")
-            h_transpose(3, 1)
-            h_copy(3, 0, "V")
-            rot_transpose(0, 0)
-            h_copy(3, 1, "S")
-            h_quant(0)
-            rot_transpose(0, 1)
-            rot_copy(0, 0, "S")
-            w_group(0, 0, "V", 16)
-            rot_copy(0, 1, "S")
-            w_group(0, 0, "S", 16)
-            rot_transpose(1, 0)
-            w_quant(0, 0)
-            rot_transpose(1, 1)
-            h_quant(1)
-            rot_copy(1, 0, "S")
-            pre_mm(0, 0)
-            rot_copy(1, 1, "S")
-            h_quant(2)
-            pre_mm(1, 0)
-            pre_mm(2, 0)
-            w_group(0, 1, "S", 80)
-            rot_quant(0)
-            pre_mm(3, 0)
-            rot_transpose(2, 0)
-            h_quant(3)
-            rot_transpose(2, 1)
-            w_group(0, 1, "V", 80)
-            rot_copy(2, 0, "S")
+            for t in range(PACK):
+                h_transpose(t, 0)
+                h_transpose(t, 1)
+                h_copy(t, 0, "S")
+                h_copy(t, 1, "V")
+            for s in range(3):
+                for half in range(2):
+                    rot_transpose(s, half)
+                    rot_copy(s, half, "S")
+                if s == 0:
+                    for c in range(D_PASSES):
+                        h_quant(c)
+                else:
+                    rot_quant(s - 1)
             base_mm(0)
-            rot_quant(1)
-            rot_copy(2, 1, "S")
-            w_quant(0, 1)
-            w_group(1, 0, "S", 48)
-            base_mm(1)
-            w_group(1, 0, "V", 48)
             base_out(0)
-            w_quant(1, 0)
-            rot_transpose(3, 0)
-            w_group(1, 1, "S", 48)
-            w_group(1, 1, "V", 48)
-            rot_transpose(3, 1)
-            base_out(1)
-            pre_mm(0, 1)
-            rot_quant(2)
-            pre_mm(1, 1)
-            rot_copy(3, 0, "S")
-            pre_mm(2, 1)
-            w_quant(1, 1)
-            base_mm(2)
-            rot_copy(3, 1, "S")
-            w_group(2, 0, "V", 48)
-            w_group(2, 0, "S", 48)
-            pre_mm(3, 1)
-            rot_quant(3)
-            rot_transpose(4, 0)
-            w_group(2, 1, "S", 32)
-            w_group(2, 1, "V", 32)
-            rot_transpose(4, 1)
-            base_out(2)
-            base_mm(3)
-            rot_copy(4, 0, "S")
-            w_quant(2, 0)
-            rot_copy(4, 1, "S")
-            w_quant(2, 1)
-            rot_transpose(5, 0)
-            base_out(3)
-            rot_quant(4)
-            rot_transpose(5, 1)
-            w_group(3, 0, "S", 32)
-            w_group(3, 0, "V", 32)
-            pre_mm(0, 2)
-            rot_copy(5, 0, "S")
-            pre_mm(1, 2)
-            pre_mm(2, 2)
-            w_group(3, 1, "V", 32)
-            rot_copy(5, 1, "S")
-            rot_transpose(6, 0)
-            w_group(3, 1, "S", 32)
-            rot_transpose(6, 1)
-            w_quant(3, 0)
-            rot_copy(6, 0, "S")
-            pre_mm(3, 2)
-            rot_quant(5)
-            pre_mm(0, 3)
-            rot_copy(6, 1, "S")
-            pre_mm(1, 3)
-            w_quant(3, 1)
-            pre_mm(2, 3)
-            pre_out(0)
+            for c in range(D_PASSES):
+                w_group(c, 0, "S", WS[c][0])
+                w_group(c, 0, "V", WS[c][0])
+                rot_quant(c + 2)
+                for half in range(2):
+                    rot_transpose(c + 3, half)
+                    rot_copy(c + 3, half, "S")
+                w_group(c, 1, "S", WS[c][1])
+                w_quant(c, 0)
+                w_group(c, 1, "V", WS[c][1])
+                base_mm(c + 1)
+                base_out(c + 1)
+                for i in range(PACK):
+                    pre_mm(i, c)
+                w_quant(c, 1)
             rot_quant(6)
+            for c in range(D_PASSES):
+                pre_mm(4, c)
             rot_transpose(7, 0)
-            pre_out(1)
             rot_transpose(7, 1)
-            diff_part(0)
+            for i in range(PACK):
+                pre_out(i)
+                if i == 2:
+                    ro_group(0, 0, "S", 64)
+                    ro_group(0, 0, "V", 64)
+                diff_part(i)
             rot_copy(7, 0, "S")
-            ro_group(0, 0, "V", 0)
-            pre_mm(3, 3)
             rot_copy(7, 1, "S")
-            pre_mm(4, 0)
-            pre_mm(4, 1)
-            pre_mm(4, 2)
-            pre_mm(4, 3)
-            pre_out(2)
-            diff_part(1)
-            pre_out(3)
-            base_mm(4)
-            diff_part(2)
-            ro_group(1, 0, "S", 128)
-            ro_group(0, 1, "V", 32)
-            base_mm(5)
-            diff_part(3)
-            pre_mm(5, 0)
-            pre_mm(5, 1)
-            pre_mm(5, 2)
-            pre_mm(5, 3)
-            ro_group(1, 1, "V", 48)
-            base_out(4)
-            rot_quant(7)
-            ro_group(0, 1, "S", 32)
-            pre_mm(6, 0)
-            pre_mm(6, 1)
-            pre_mm(6, 2)
-            pre_mm(6, 3)
-            diff_group(0)
             pre_out(4)
-            ro_group(1, 1, "S", 48)
-            base_mm(6)
-            ro_quant(0, 0)
-            base_out(5)
-            diff_part(4)
-            base_mm(7)
-            ro_quant(1, 0)
+            ro_group(1, 0, "S", 64)
+            ro_group(1, 0, "V", 64)
+            for c in range(D_PASSES):
+                pre_mm(5, c)
+            base_mm(5)
             pre_out(5)
-            pre_out(6)
-            diff_quant(0)
-            pre_mm(7, 0)
-            pre_mm(7, 1)
-            pre_mm(7, 2)
-            pre_mm(7, 3)
+            base_out(5)
+            diff_group(0)
+            rot_quant(7)
+            ro_group(0, 1, "S", 80)
+            ro_group(0, 1, "V", 80)
+            base_mm(6)
+            for c in range(D_PASSES):
+                pre_mm(6, c)
             base_out(6)
+            pre_out(6)
+            diff_part(4)
             diff_part(5)
+            diff_quant(0)
+            base_mm(7)
+            for c in range(D_PASSES):
+                pre_mm(7, c)
             base_out(7)
-            ro_quant(0, 1)
-            out_mm(0, 0, 0)
-            out_mm(0, 1, 0)
             pre_out(7)
+            for q, n in ((0, 0), (1, 0), (0, 1)):
+                ro_quant(q, n)
             diff_part(6)
-            out_mm(0, 2, 0)
-            out_mm(0, 3, 0)
-            ro_group(0, 2, "S", 128)
             diff_part(7)
-            out_mm(1, 0, 0)
-            out_mm(1, 1, 0)
             diff_group(1)
-            out_mm(1, 2, 0)
-            out_mm(1, 3, 0)
+            ro_group(1, 1, "S", 64)
             diff_quant(1)
-            ro_group(1, 2, "S", 64)
-            ro_group(1, 2, "V", 64)
-            out_mm(0, 0, 1)
-            out_mm(0, 1, 1)
-            ro_group(0, 3, "V", 16)
-            out_mm(0, 2, 1)
-            out_copy(0, 0, "S")
-            out_mm(0, 3, 1)
-            out_copy(0, 1, "S")
+            ro_group(0, 2, "S", 64)
+            ro_group(1, 2, "S", 80)
+            ro_group(1, 1, "V", 64)
+            ro_group(0, 2, "V", 64)
             ro_quant(1, 1)
-            out_copy(0, 2, "S")
+            ro_group(1, 2, "V", 80)
             ro_quant(0, 2)
-            out_mm(1, 0, 1)
-            out_copy(0, 3, "S")
-            out_mm(1, 1, 1)
             ro_quant(1, 2)
-            out_mm(1, 2, 1)
-            out_copy(1, 0, "S")
-            out_mm(1, 3, 1)
-            out_group(0)
-            out_mm(2, 0, 0)
-            out_copy(1, 1, "S")
-            out_mm(2, 0, 1)
-            out_mm(2, 1, 0)
-            out_copy(1, 2, "S")
-            out_mm(2, 1, 1)
-            out_mm(2, 2, 0)
-            ro_group(1, 3, "V", 24)
-            out_copy(1, 3, "S")
-            out_mm(2, 2, 1)
-            out_mm(2, 3, 0)
-            out_copy(2, 0, "S")
-            out_mm(2, 3, 1)
-            out_quant(0)
+            for n in range(2):
+                for t in range(PACK):
+                    out_mm(n, t, 0)
+            for t in range(PACK):
+                out_mm(0, t, 1)
+                out_copy(0, t, "S")
             ro_group(0, 3, "S", 16)
-            ro_group(1, 3, "S", 24)
+            ro_group(0, 3, "V", 16)
+            for t in range(PACK):
+                out_mm(1, t, 1)
+                out_copy(1, t, "S")
+            ro_group(1, 3, "S", 0)
+            ro_group(1, 3, "V", 0)
             ro_quant(0, 3)
-            out_copy(2, 1, "S")
             ro_quant(1, 3)
-            out_mm(3, 0, 0)
-            out_copy(2, 2, "S")
-            out_group(1)
-            out_mm(3, 0, 1)
-            out_mm(3, 1, 0)
-            out_copy(2, 3, "S")
-            out_mm(3, 1, 1)
-            out_mm(3, 2, 0)
-            out_mm(3, 2, 1)
-            out_mm(3, 3, 0)
-            out_copy(3, 0, "S")
-            out_mm(3, 3, 1)
-            out_mm(4, 0, 0)
-            out_group(2)
-            out_copy(3, 1, "S")
-            out_mm(4, 0, 1)
-            out_mm(4, 1, 0)
-            out_copy(3, 2, "S")
-            out_mm(4, 1, 1)
-            out_mm(4, 2, 0)
-            out_copy(3, 3, "S")
-            out_mm(4, 2, 1)
-            out_mm(4, 3, 0)
-            out_copy(4, 0, "S")
-            out_mm(4, 3, 1)
-            out_quant(1)
-            out_copy(4, 1, "S")
-            out_copy(4, 2, "S")
-            out_group(3)
-            out_copy(4, 3, "S")
-            out_quant(2)
-            out_group(4)
-            out_quant(3)
-            out_quant(4)
+            for n in range(2, len(CHUNKS)):
+                for t in range(PACK):
+                    out_mm(n, t, 0)
+                    out_mm(n, t, 1)
+                    out_copy(n, t, "S")
+                out_group(n - 2, "S", OS[n - 2])
+                out_group(n - 2, "V", OS[n - 2])
+                if n >= 3:
+                    out_quant(n - 3)
+            for n in range(len(CHUNKS) - 2, len(CHUNKS)):
+                out_group(n, "S", OS[n])
+                out_group(n, "V", OS[n])
+                out_quant(n - 1)
+            out_quant(len(CHUNKS) - 1)
             scales_store(0, D)

@@ -32,12 +32,12 @@ def tile_loreftsubspaceintervention_x1_kernel(tc, h, rot_in, w, b, g, rot_out, p
     with ExitStack() as ctx:
         const = ctx.enter_context(tc.tile_pool(name="const", bufs=1))
         keep = ctx.enter_context(tc.tile_pool(name="keep", bufs=1))
-        rows = ctx.enter_context(tc.tile_pool(name="rows", bufs=6))
+        rows = ctx.enter_context(tc.tile_pool(name="rows", bufs=10))
         wide = ctx.enter_context(tc.tile_pool(name="wide", bufs=4))
-        grouped = ctx.enter_context(tc.tile_pool(name="grouped", bufs=10))
+        grouped = ctx.enter_context(tc.tile_pool(name="grouped", bufs=8))
         rot_pool = ctx.enter_context(tc.tile_pool(name="rot_pool", bufs=4))
-        src_pool = ctx.enter_context(tc.tile_pool(name="src_pool", bufs=4))
-        base_pool = ctx.enter_context(tc.tile_pool(name="base_pool", bufs=8))
+        src_pool = ctx.enter_context(tc.tile_pool(name="src_pool", bufs=3))
+        base_pool = ctx.enter_context(tc.tile_pool(name="base_pool", bufs=6))
         big = ctx.enter_context(tc.tile_pool(name="big", bufs=4))
         psum_t = ctx.enter_context(tc.psum_pool(name="psum_t", bufs=2))
         psum_m = ctx.enter_context(tc.psum_pool(name="psum_m", bufs=6))
@@ -351,8 +351,8 @@ def tile_loreftsubspaceintervention_x1_kernel(tc, h, rot_in, w, b, g, rot_out, p
                     out=out_2[0][4 * q : 4 * q + 4, lo:hi].bitcast(I32), in_=o_scales[32 * q : 32 * q + 4, lo:hi].bitcast(I32)
                 )
 
-        WS = [[0, 24], [40, 40], [40, 40], [40, 32]]
-        OS = [0,0,0,48]
+        WS = [[32, 32], [56, 40], [40, 40], [64, 16]]
+        OS = [0,0,64,64]
         with tc.manual_schedule():
             for t in range(PACK):
                 h_transpose(t, 0)
@@ -373,15 +373,15 @@ def tile_loreftsubspaceintervention_x1_kernel(tc, h, rot_in, w, b, g, rot_out, p
             for c in range(D_PASSES):
                 w_group(c, 0, "S", WS[c][0])
                 w_group(c, 0, "V", WS[c][0])
+                base_mm(c + 1)
+                base_out(c + 1)
+                w_group(c, 1, "S", WS[c][1])
+                w_group(c, 1, "V", WS[c][1])
+                w_quant(c, 0)
                 rot_quant(c + 2)
                 for half in range(2):
                     rot_transpose(c + 3, half)
                     rot_copy(c + 3, half, "S")
-                w_group(c, 1, "S", WS[c][1])
-                w_quant(c, 0)
-                w_group(c, 1, "V", WS[c][1])
-                base_mm(c + 1)
-                base_out(c + 1)
                 for i in range(PACK):
                     pre_mm(i, c)
                 w_quant(c, 1)
@@ -393,8 +393,8 @@ def tile_loreftsubspaceintervention_x1_kernel(tc, h, rot_in, w, b, g, rot_out, p
             for i in range(PACK):
                 pre_out(i)
                 if i == 2:
-                    ro_group(0, 0, "S", 64)
-                    ro_group(0, 0, "V", 64)
+                    ro_group(0, 0, "S", 40)
+                    ro_group(0, 0, "V", 40)
                 diff_part(i)
             rot_copy(7, 0, "S")
             rot_copy(7, 1, "S")
@@ -408,8 +408,8 @@ def tile_loreftsubspaceintervention_x1_kernel(tc, h, rot_in, w, b, g, rot_out, p
             base_out(5)
             diff_group(0)
             rot_quant(7)
-            ro_group(0, 1, "S", 80)
-            ro_group(0, 1, "V", 80)
+            ro_group(0, 1, "S", 64)
+            ro_group(0, 1, "V", 64)
             base_mm(6)
             for c in range(D_PASSES):
                 pre_mm(6, c)
@@ -430,10 +430,10 @@ def tile_loreftsubspaceintervention_x1_kernel(tc, h, rot_in, w, b, g, rot_out, p
             diff_group(1)
             ro_group(1, 1, "S", 64)
             diff_quant(1)
-            ro_group(0, 2, "S", 64)
+            ro_group(0, 2, "S", 56)
             ro_group(1, 2, "S", 80)
             ro_group(1, 1, "V", 64)
-            ro_group(0, 2, "V", 64)
+            ro_group(0, 2, "V", 56)
             ro_quant(1, 1)
             ro_group(1, 2, "V", 80)
             ro_quant(0, 2)
@@ -444,8 +444,8 @@ def tile_loreftsubspaceintervention_x1_kernel(tc, h, rot_in, w, b, g, rot_out, p
             for t in range(PACK):
                 out_mm(0, t, 1)
                 out_copy(0, t, "S")
-            ro_group(0, 3, "S", 16)
-            ro_group(0, 3, "V", 16)
+            ro_group(0, 3, "S", 0)
+            ro_group(0, 3, "V", 0)
             for t in range(PACK):
                 out_mm(1, t, 1)
                 out_copy(1, t, "S")

from contextlib import ExitStack

import concourse.mybir as mybir
from concourse.masks import make_identity

T, D, R = 512, 2048, 1024

FLOPS = 2 * T * D * R * 3

F32 = mybir.dt.float32
BF16 = mybir.dt.bfloat16
U32 = mybir.dt.uint32
I32 = mybir.dt.int32
U8 = mybir.dt.uint8
FP8X4 = mybir.dt.float8_e4m3fn_x4
ACT = mybir.ActivationFunctionType
ALU = mybir.AluOpType

P = 128
PACK = 4
K_PASS = P * PACK
D_PASSES = D // K_PASS
R_PASSES = R // K_PASS
N_TILE = 512
N_CHUNKS = D // N_TILE
R_TILES = R // P
CHUNKS = ((0,512),(512,1024),(1024,1536),(1536,2048))


def tile_loreftsubspaceintervention_x1_kernel(tc, h, rot_in, w, b, g, rot_out, pw, out_0, out_1, out_2):
    nc = tc.nc
    with ExitStack() as ctx:
        const = ctx.enter_context(tc.tile_pool(name="const", bufs=1))
        keep = ctx.enter_context(tc.tile_pool(name="keep", bufs=1))
        rows = ctx.enter_context(tc.tile_pool(name="rows", bufs=10))
        wide = ctx.enter_context(tc.tile_pool(name="wide", bufs=4))
        grouped = ctx.enter_context(tc.tile_pool(name="grouped", bufs=8))
        rot_pool = ctx.enter_context(tc.tile_pool(name="rot_pool", bufs=4))
        src_pool = ctx.enter_context(tc.tile_pool(name="src_pool", bufs=3))
        base_pool = ctx.enter_context(tc.tile_pool(name="base_pool", bufs=6))
        big = ctx.enter_context(tc.tile_pool(name="big", bufs=4))
        psum_t = ctx.enter_context(tc.psum_pool(name="psum_t", bufs=2))
        psum_m = ctx.enter_context(tc.psum_pool(name="psum_m", bufs=6))

        ident = const.tile([P, P], F32, name="ident")
        make_identity(nc, ident[:])

        h_view = h.rearrange("(m t) k -> t m k", t=PACK)
        rot_view = rot_in.rearrange("(g m t) k -> g t m k", g=R_PASSES, t=PACK)

        def load_rows(view):
            row = rows.tile([P, D], BF16, name="row")
            nc.sync.dma_start(out=row[:], in_=view)
            return row

        b_raw = const.tile([P, R_PASSES, PACK], BF16, name="b_raw")
        g_raw = const.tile([P, R_PASSES, PACK], BF16, name="g_raw")
        pw_raw = const.tile([P, PACK], BF16, name="pw_raw")
        nc.scalar.dma_start(out=g_raw[:], in_=g.rearrange("(g m t) -> m g t", g=R_PASSES, t=PACK))
        nc.scalar.dma_start(out=b_raw[:], in_=b.rearrange("(g m t) -> m g t", g=R_PASSES, t=PACK))
        nc.scalar.dma_start(out=pw_raw[:], in_=pw.rearrange("(m t) -> m t", t=PACK))
        b_col = const.tile([P, R_PASSES, PACK], F32, name="b_col")
        g_col = const.tile([P, R_PASSES, PACK], F32, name="g_col")
        pw_col = const.tile([P, PACK], F32, name="pw_col")
        warm = const.tile([P, 1], F32, name="warm")
        nc.gpsimd.memset(warm[:], 0.0)
        nc.scalar.activation(out=warm[:], in_=warm[:], func=ACT.Silu)
        nc.gpsimd.tensor_copy(out=g_col[:], in_=g_raw[:])
        nc.gpsimd.tensor_copy(out=b_col[:], in_=b_raw[:])
        nc.gpsimd.tensor_copy(out=pw_col[:], in_=pw_raw[:])

        h_rows = {}
        rot_rows = {}
        w_raw = {}
        ro_raw = {}

        def load_h(t):
            h_rows[t] = load_rows(h_view[t])

        def load_rot(s):
            rot_rows[s] = load_rows(rot_view[s // PACK, s % PACK])

        def load_w(c):
            raw = wide.tile([P, PACK, R], BF16, name="raw")
            nc.sync.dma_start(out=raw[:], in_=w[c * K_PASS : (c + 1) * K_PASS, :].rearrange("(p j) r -> p j r", j=PACK))
            for gi in range(R_PASSES):
                w_raw[c, gi] = raw[:, :, gi * K_PASS : (gi + 1) * K_PASS]

        def load_w_half(c, gi):
            row = rows.tile([P, PACK, K_PASS], BF16, name="row")
            nc.sync.dma_start(
                out=row[:], in_=w[c * K_PASS : (c + 1) * K_PASS, gi * K_PASS : (gi + 1) * K_PASS].rearrange("(p j) r -> p j r", j=PACK)
            )
            w_raw[c, gi] = row[:]

        def load_ro(q, half):
            ro_raw[q, half] = wide.tile([P, PACK, 1024], BF16, name="raw")
            nc.sync.dma_start(
                out=ro_raw[q, half][:],
                in_=rot_out[q * K_PASS : (q + 1) * K_PASS, half * 1024 : (half + 1) * 1024].rearrange("(p j) n -> p j n", j=PACK),
            )

        for t in range(PACK):
            load_h(t)
        load_rot(0)
        load_rot(1)
        for c in range(D_PASSES):
            load_rot(c + 2)
            load_w(c)
        load_rot(6)
        load_rot(7)
        for half in range(2):
            for q in range(R_PASSES):
                load_ro(q, half)

        h_codes = keep.tile([P, D_PASSES, T], U32, name="h_codes", align_bytes=64)
        h_scales = keep.tile([P, D_PASSES, T], U8, name="h_scales", align_bytes=64)
        w_codes = keep.tile([P, D_PASSES, R], U32, name="w_codes", align_bytes=64)
        w_scales = keep.tile([P, D_PASSES, R], U8, name="w_scales", align_bytes=64)
        ro_codes = keep.tile([P, R_PASSES, D], U32, name="ro_codes", align_bytes=64)
        ro_scales = keep.tile([P, R_PASSES, D], U8, name="ro_scales", align_bytes=64)
        d_codes = keep.tile([P, R_PASSES, T], U32, name="d_codes", align_bytes=64)
        d_scales = keep.tile([P, R_PASSES, T], U8, name="d_scales", align_bytes=64)
        o_codes = keep.tile([P, D], U32, name="o_codes", align_bytes=64)
        o_scales = keep.tile([P, D], U8, name="o_scales", align_bytes=64)

        def group_tile():
            grp = grouped.tile([P, N_TILE, PACK], BF16, name="grp", align_bytes=64)
            return grp

        def quantize(codes, scales, grp):
            nc.vector.quantize_mx(out=codes.bitcast(FP8X4), scales=scales, in_=grp[:].rearrange("p w j -> p (w j)"))

        def copy(eng, out, in_):
            if eng == "S":
                nc.scalar.copy(out=out, in_=in_)
            else:
                nc.vector.tensor_copy(out=out, in_=in_)

        h_grp = {}

        def t_words(bank, slot, row, c):
            words = row[:].bitcast(F32)
            for u in range(2):
                nc.tensor.transpose(bank[:, slot, u, :], words[:, 256 * c + u : 256 * (c + 1) : 2], ident[:])

        def t_bank(kind):
            if kind == "t":
                bank = psum_t.tile([P, 2, 2, P], F32, name="bank_t")
            else:
                bank = psum_m.tile([P, 2, 2, P], F32, name="bank_m")
            return bank

        def copy_words(eng, grp, off, bank):
            dst = grp[:].rearrange("p w j -> p (w j)").bitcast(F32).rearrange("p (s r u) -> p s r u", r=P, u=2)
            copy(eng, dst[:, off : off + 2], bank[:].rearrange("p s u r -> p s r u"))

        banks = {}

        def h_transpose(t, cp):
            bank = t_bank("m")
            for i in range(2):
                c = 2 * cp + i
                if c not in h_grp:
                    h_grp[c] = group_tile()
                t_words(bank, i, h_rows[t], c)
            banks["h", t, cp] = bank

        def h_copy(t, cp, eng):
            bank = banks["h", t, cp]
            for i in range(2):
                dst = h_grp[2 * cp + i][:].rearrange("p w j -> p (w j)").bitcast(F32).rearrange("p (s r u) -> p s r u", r=P, u=2)
                copy(eng, dst[:, t], bank[:, i].rearrange("p u r -> p r u"))

        def h_quant(c):
            quantize(h_codes[:, c, :], h_scales[:, c, :], h_grp[c])

        rot_grp = {}
        rot_codes = {}

        def rot_transpose(s, half):
            if half == 0:
                rot_grp[s] = group_tile()
            bank = t_bank("t")
            for i in range(2):
                t_words(bank, i, rot_rows[s], 2 * half + i)
            banks["r", s, half] = bank

        def rot_copy(s, half, eng):
            copy_words(eng, rot_grp[s], 2 * half, banks["r", s, half])

        def rot_quant(s):
            codes = rot_pool.tile([P, D_PASSES, P], U32, name="r_codes", align_bytes=64)
            scales = rot_pool.tile([P, D_PASSES, P], U8, name="r_scales", align_bytes=64)
            quantize(codes[:].rearrange("p c m -> p (c m)"), scales[:].rearrange("p c m -> p (c m)"), rot_grp[s])
            rot_codes[s] = (codes, scales)

        w_grp = {}

        def w_group(c, gi, eng, s_part):
            if (c, gi) not in w_grp:
                w_grp[c, gi] = group_tile()
            dst = w_grp[c, gi][:].rearrange("p (t m) j -> p t m j", t=PACK)
            source = w_raw[c, gi].rearrange("p j (m t) -> p t m j", t=PACK)
            cols = slice(0, P - s_part) if eng == "V" else slice(P - s_part, P)
            if cols.start < cols.stop:
                copy(eng, dst[:, :, cols], source[:, :, cols])

        def w_quant(c, gi):
            cols = slice(gi * 512, (gi + 1) * 512)
            quantize(w_codes[:, c, cols], w_scales[:, c, cols], w_grp[c, gi])

        ro_grp = {}

        def ro_group(q, n, eng, s_part):
            if (q, n) not in ro_grp:
                ro_grp[q, n] = group_tile()
            lo = (n % 2) * 512
            dst = ro_grp[q, n][:].rearrange("p (c i) j -> p c j i", i=4)
            source = ro_raw[q, n // 2][:, :, lo : lo + 512].rearrange("p j (c i) -> p c j i", i=4)
            cols = slice(0, P - s_part) if eng == "V" else slice(P - s_part, P)
            if cols.start < cols.stop:
                copy(eng, dst[:, cols], source[:, cols])

        def ro_quant(q, n):
            cols = slice(n * 512, (n + 1) * 512)
            quantize(ro_codes[:, q, cols], ro_scales[:, q, cols], ro_grp[q, n])

        def mm(acc, lhs, lhs_s, rhs, rhs_s, start, stop):
            nc.tensor.matmul_mx(
                out=acc, lhsT=lhs.bitcast(FP8X4), lhsT_scale=lhs_s, rhs=rhs.bitcast(FP8X4), rhs_scale=rhs_s, start=start, stop=stop
            )

        base = {}
        src = {}
        accs = {}

        def mm_bank():
            acc = psum_m.tile([P, N_TILE], F32, name="bank_m")
            return acc

        def base_mm(s):
            acc = mm_bank()
            codes, scales = rot_codes[s]
            for c in range(D_PASSES):
                mm(acc[:], codes[:, c, :], scales[:, c, :], h_codes[:, c, :], h_scales[:, c, :], c == 0, c == D_PASSES - 1)
            accs["b", s] = acc

        def base_out(s):
            base[s] = base_pool.tile([P, T], F32, name="base")
            nc.scalar.activation(out=base[s][:], in_=accs["b", s][:], func=ACT.Copy, scale=g_col[:, s // PACK, s % PACK : s % PACK + 1])

        def pre_mm(s, c):
            if c == 0:
                accs["p", s] = mm_bank()
            cols = slice(s * P, (s + 1) * P)
            mm(accs["p", s][:], w_codes[:, c, cols], w_scales[:, c, cols], h_codes[:, c, :], h_scales[:, c, :], c == 0, c == D_PASSES - 1)

        def pre_out(s):
            src[s] = src_pool.tile([P, T], F32, name="src")
            nc.scalar.activation(out=src[s][:], in_=accs["p", s][:], func=ACT.Silu, bias=b_col[:, s // PACK, s % PACK : s % PACK + 1])

        diff = {}

        def diff_part(s):
            gi, t = divmod(s, PACK)
            if t == 0:
                diff[gi] = big.tile([P, PACK, T], F32, name="big_t")
            nc.vector.scalar_tensor_tensor(
                out=diff[gi][:, t, :], in0=src[s][:], scalar=g_col[:, gi, t : t + 1], in1=base[s][:], op0=ALU.mult, op1=ALU.subtract
            )

        d_grp = {}

        def diff_group(gi):
            d_grp[gi] = group_tile()
            nc.vector.tensor_copy(
                out=d_grp[gi][:].rearrange("p (c i) j -> p c j i", i=4),
                in_=diff[gi][:].rearrange("p j (c i) -> p c j i", i=4),
            )

        def diff_quant(gi):
            quantize(d_codes[:, gi, :], d_scales[:, gi, :], d_grp[gi])

        out_view = out_0.rearrange("(m t) d -> m t d", t=PACK)
        words_view = out_1[0]
        res = {}
        n_alloc = [0]

        def out_mm(n, t, q):
            lo, hi = CHUNKS[n]
            if q == 0:
                use_t = n_alloc[0] % 8 >= 6
                n_alloc[0] += 1
                if use_t:
                    acc = psum_t.tile([P, N_TILE], F32, name="bank_t")
                else:
                    acc = mm_bank()
                accs["o", n, t] = acc
            mm(
                accs["o", n, t][:, : hi - lo],
                d_codes[:, q, t * P : (t + 1) * P],
                d_scales[:, q, t * P : (t + 1) * P],
                ro_codes[:, q, lo:hi],
                ro_scales[:, q, lo:hi],
                q == 0,
                q == R_PASSES - 1,
            )

        def out_copy(n, t, eng):
            lo, hi = CHUNKS[n]
            if n not in res:
                res[n] = big.tile([P, PACK, N_TILE], F32, name="big_t")
            dst = res[n][:, t, : hi - lo]
            acc = accs["o", n, t][:, : hi - lo]
            if eng == "S":
                nc.scalar.activation(out=dst, in_=acc, func=ACT.Copy, scale=pw_col[:, t : t + 1])
            else:
                nc.vector.tensor_scalar(out=dst, in0=acc, scalar1=pw_col[:, t : t + 1], scalar2=None, op0=ALU.mult)
            done = out_done.setdefault(n, [])
            done.append(t)
            if len(done) in (2, 4) and sorted(done[-2:]) in ([0, 1], [2, 3]):
                t0 = min(done[-2:])
                nc.sync.dma_start(out=out_view[:, t0 : t0 + 2, lo:hi], in_=res[n][:, t0 : t0 + 2, : hi - lo])
            elif len(done) == 4:
                nc.sync.dma_start(out=out_view[:, :, lo:hi], in_=res[n][:, :, : hi - lo])

        out_done = {}
        o_grp = {}

        def out_group(n, eng, s_part):
            lo, hi = CHUNKS[n]
            if n not in o_grp:
                o_grp[n] = group_tile()
            dst = o_grp[n][:, : hi - lo].rearrange("p (c i) j -> p c j i", i=4)
            source = res[n][:, :, : hi - lo].rearrange("p j (c i) -> p c j i", i=4)
            cols = slice(0, P - s_part) if eng == "V" else slice(P - s_part, P)
            if cols.start < cols.stop:
                copy(eng, dst[:, cols], source[:, cols])

        def out_quant(n):
            lo, hi = CHUNKS[n]
            nc.vector.quantize_mx(
                out=o_codes[:, lo:hi].bitcast(FP8X4), scales=o_scales[:, lo:hi], in_=o_grp[n][:, : hi - lo].rearrange("p w j -> p (w j)")
            )
            nc.sync.dma_start(out=words_view[:, lo:hi, :].rearrange("p m t -> p (m t)").bitcast(I32), in_=o_codes[:, lo:hi].bitcast(I32))

        def scales_store(lo, hi):
            for q in range(4):
                nc.sync.dma_start(
                    out=out_2[0][4 * q : 4 * q + 4, lo:hi].bitcast(I32), in_=o_scales[32 * q : 32 * q + 4, lo:hi].bitcast(I32)
                )

        WS = [[32, 32], [56, 40], [40, 40], [64, 16]]
        OS = [0,0,64,64]
        with tc.manual_schedule():
            for t in range(PACK):
                h_transpose(t, 0)
                h_transpose(t, 1)
                h_copy(t, 0, "S")
                h_copy(t, 1, "V")
            for s in range(3):
                for half in range(2):
                    rot_transpose(s, half)
                    rot_copy(s, half, "S")
                if s == 0:
                    for c in range(D_PASSES):
                        h_quant(c)
                else:
                    rot_quant(s - 1)
            base_mm(0)
            base_out(0)
            for c in range(D_PASSES):
                w_group(c, 0, "S", WS[c][0])
                w_group(c, 0, "V", WS[c][0])
                base_mm(c + 1)
                base_out(c + 1)
                w_group(c, 1, "S", WS[c][1])
                w_group(c, 1, "V", WS[c][1])
                w_quant(c, 0)
                rot_quant(c + 2)
                for half in range(2):
                    rot_transpose(c + 3, half)
                    rot_copy(c + 3, half, "S")
                for i in range(PACK):
                    pre_mm(i, c)
                w_quant(c, 1)
            rot_quant(6)
            for c in range(D_PASSES):
                pre_mm(4, c)
            rot_transpose(7, 0)
            rot_transpose(7, 1)
            for i in range(PACK):
                pre_out(i)
                if i == 2:
                    ro_group(0, 0, "S", 40)
                    ro_group(0, 0, "V", 40)
                diff_part(i)
            rot_copy(7, 0, "S")
            rot_copy(7, 1, "S")
            pre_out(4)
            ro_group(1, 0, "S", 64)
            ro_group(1, 0, "V", 64)
            for c in range(D_PASSES):
                pre_mm(5, c)
            base_mm(5)
            pre_out(5)
            base_out(5)
            diff_group(0)
            rot_quant(7)
            ro_group(0, 1, "S", 64)
            ro_group(0, 1, "V", 64)
            base_mm(6)
            for c in range(D_PASSES):
                pre_mm(6, c)
            base_out(6)
            pre_out(6)
            diff_part(4)
            diff_part(5)
            diff_quant(0)
            base_mm(7)
            for c in range(D_PASSES):
                pre_mm(7, c)
            base_out(7)
            pre_out(7)
            for q, n in ((0, 0), (1, 0), (0, 1)):
                ro_quant(q, n)
            diff_part(6)
            diff_part(7)
            diff_group(1)
            ro_group(1, 1, "S", 64)
            diff_quant(1)
            ro_group(0, 2, "S", 56)
            ro_group(1, 2, "S", 80)
            ro_group(1, 1, "V", 64)
            ro_group(0, 2, "V", 56)
            ro_quant(1, 1)
            ro_group(1, 2, "V", 80)
            ro_quant(0, 2)
            ro_quant(1, 2)
            for n in range(2):
                for t in range(PACK):
                    out_mm(n, t, 0)
            for t in range(PACK):
                out_mm(0, t, 1)
                out_copy(0, t, "S")
            ro_group(0, 3, "S", 0)
            ro_group(0, 3, "V", 0)
            for t in range(PACK):
                out_mm(1, t, 1)
                out_copy(1, t, "S")
            ro_group(1, 3, "S", 0)
            ro_group(1, 3, "V", 0)
            ro_quant(0, 3)
            ro_quant(1, 3)
            for n in range(2, len(CHUNKS)):
                for t in range(PACK):
                    out_mm(n, t, 0)
                    out_mm(n, t, 1)
                    out_copy(n, t, "S")
                out_group(n - 2, "S", OS[n - 2])
                out_group(n - 2, "V", OS[n - 2])
                if n >= 3:
                    out_quant(n - 3)
            for n in range(len(CHUNKS) - 2, len(CHUNKS)):
                out_group(n, "S", OS[n])
                out_group(n, "V", OS[n])
                out_quant(n - 1)
            out_quant(len(CHUNKS) - 1)
            scales_store(0, D)
